import numpy as np
import ml_dtypes


def mxq(x, axis, fmt="e4m3"):
    dtype, down = {"e4m3": (ml_dtypes.float8_e4m3fn, 7), "e5m2": (ml_dtypes.float8_e5m2, 14)}[fmt]
    v = np.moveaxis(np.asarray(x, np.float32).astype(ml_dtypes.bfloat16).astype(np.float64), axis, -1)
    blocks = v.reshape(v.shape[:-1] + (-1, 32))
    amax = np.abs(blocks).max(-1, keepdims=True)
    byte = np.maximum(np.where(amax > 0, np.frexp(amax)[1] - 1 + 127, 0) - down, 1)
    scale = np.exp2(byte - 127.0)
    codes = (blocks / scale).astype(np.float32).astype(dtype).astype(np.float64)
    return np.moveaxis((codes * scale).reshape(v.shape), -1, axis)


WIDE = False


def mx_kscale(k):
    if not WIDE:
        return np.ones(k)
    levels = np.array([10, -10, 5, -5, 0])
    if k % 512:
        return np.exp2(np.random.permutation(np.resize(levels, k // 32))).repeat(32)
    a = np.empty((k // 512, 16))
    for p in range(k // 512):
        a[p, :8] = np.random.permutation(np.resize(levels, 8))
        for g in range(8):
            far = levels[np.abs(levels - a[p, g]) >= 10]
            a[p, g + 8] = far[np.random.randint(len(far))]
    return np.exp2(a.ravel()).repeat(32)


def f64(x):
    return np.asarray(x).astype(np.float64)


def striped(idx):
    return np.tile(idx.reshape(-1, 16).T, (8, 1)).astype(np.uint16)


def unstriped(offs):
    return offs[:16].T.reshape(-1).astype(np.int64)


def striped8(idx):
    return np.concatenate([x.reshape(-1, 16).T for x in idx]).astype(np.uint16)


def runs(offs, k):
    lists = np.stack([offs[16 * r : 16 * r + 16].T.reshape(-1) for r in range(8)]).astype(np.int64)
    return lists[np.arange(k) % 512 // 64]


def pack_weight(w):
    k, n = w.shape
    w = f64(np.asarray(w, np.float32).astype(ml_dtypes.bfloat16)).reshape(k // 32, 32, n)
    amax = np.abs(w).max(1)
    byte = np.clip(np.where(amax > 0, np.frexp(amax)[1] - 1 + 127 - 7, 1), 1, 254)
    scaled = (w * np.exp2(127.0 - byte)[:, None, :]).reshape(k, n).astype(np.float32)
    words = np.ascontiguousarray(scaled.reshape(k // 512, 128, 4, n).transpose(0, 1, 3, 2)).astype(ml_dtypes.float8_e4m3fn).view(np.uint8)
    return words, np.ascontiguousarray(byte.astype(np.uint8).reshape(k // 512, 16, n))


def unpack_weight(words, scales):
    g, p, n, _ = words.shape
    vals = np.ascontiguousarray(words).view(ml_dtypes.float8_e4m3fn).astype(np.float64) * np.repeat(np.exp2(scales.astype(np.float64) - 127.0), 8, axis=1)[..., None]
    return vals.transpose(0, 1, 3, 2).reshape(g * 512, n)


def sigmoid(v):
    return 1.0 / (1.0 + np.exp(-np.maximum(v, -700.0)))


K, T, S, N = 1024, 2048, 512, 512


def setup_inputs():
    n = np.random.standard_normal
    s = mx_kscale(K)[:, None]
    packed_xT = pack_weight(n((K, T)) * s)
    return {
        "x_words": packed_xT[0],
        "x_scales": packed_xT[1],
        "cell": n((N, S)).astype(np.float32),
        "w1": (n((K, N)) / np.sqrt(K) / s).astype(np.float32),
        "w2": (n((K, N)) / np.sqrt(K) / s).astype(np.float32),
        "w3": (n((K, N)) / np.sqrt(K) / s).astype(np.float32),
        "hw": n((N, S)).astype(np.float32),
        "offs": striped(np.random.permutation(T)[:S]),
        "par": striped8(np.random.randint(0, S, (8, S))),
    }


def reference(x_words, x_scales, cell, w1, w2, w3, hw, offs, par):
    xq = unpack_weight(x_words, x_scales)[:, unstriped(offs)]
    rg = sigmoid(mxq(f64(w3), 0, "e4m3").T @ xq)
    y = mxq(f64(w1), 0, "e4m3").T @ xq
    fg = sigmoid(mxq(f64(w2), 0, "e4m3").T @ xq)
    c0 = f64(cell)[np.arange(N)[:, None], runs(par, N)]
    cn = y + fg * (c0 - y)
    return f64(hw) + rg * (np.tanh(cn) - f64(hw))

@@ -1,0 +1,228 @@
+from contextlib import ExitStack
+
+import concourse.mybir as mybir
+from concourse.masks import make_identity
+
+K, T, S, N = 1024, 2048, 512, 512
+FLOPS = 3 * 2 * K * S * N
+
+F32 = mybir.dt.float32
+BF16 = mybir.dt.bfloat16
+I32 = mybir.dt.int32
+U32 = mybir.dt.uint32
+U16 = mybir.dt.uint16
+U8 = mybir.dt.uint8
+FP8X4 = mybir.dt.float8_e4m3fn_x4
+ALU = mybir.AluOpType
+ACT = mybir.ActivationFunctionType
+
+P = 128
+PACK = 4
+K_PASS = P * PACK
+PASSES = K // K_PASS
+HALVES = 2
+HALF = N // HALVES
+BLOCKS = S // P
+CELL_TILES = N // P
+RUN = 4
+LIST_COLS = S // 16
+
+
+def tile_picked_sru8_none_p_kernel(tc, x_words, x_scales, cell, w1, w2, w3, hw, offs, par, out):
+    nc = tc.nc
+    with ExitStack() as ctx:
+        sb = ctx.enter_context(tc.tile_pool(name="sb", bufs=1))
+        ps = ctx.enter_context(tc.psum_pool(name="ps", bufs=1))
+
+        def tile(name, shape, dtype):
+            return sb.tile(shape, dtype, name=name, align_bytes=64)
+
+        def bank(name, tag, shape):
+            return ps.tile(shape, F32, name=name, tag=tag)
+
+        par_t = sb.tile([P, LIST_COLS], U16, name="par_t")
+        offs_t = sb.tile([P, LIST_COLS], U16, name="offs_t")
+
+        scale_win = tile("scale_win", [P, T], U8)
+        nc.vector.memset(scale_win[:].bitcast(I32), 0)
+        for q in range(4):
+            nc.scalar.dma_start(
+                out=scale_win[32 * q : 32 * q + 4 * PASSES, :].bitcast(I32),
+                in_=x_scales[:, 4 * q : 4 * q + 4, :].bitcast(I32),
+            )
+        ident = tile("ident", [P, P], F32)
+        make_identity(nc, ident[:])
+
+        warm_in = tile("warm_in", [P, 1], F32)
+        warm_out = tile("warm_out", [P, 1], F32)
+        nc.vector.memset(warm_in[:], 0.0)
+        nc.scalar.activation(warm_out[:], warm_in[:], ACT.Sigmoid)
+
+        nc.sync.dma_start(par_t[:], par)
+        cell_rows = cell.rearrange("(g t e) j -> t g e j", t=CELL_TILES, e=RUN)
+        cell_win = []
+        for t in range(CELL_TILES):
+            win = tile("cell_win%d" % t, [P, S], F32)
+            nc.sync.dma_start(out=win[:], in_=cell_rows[t])
+            cell_win.append(win)
+        nc.sync.dma_start(offs_t[:], offs)
+
+        word_win = [tile("word_win%d" % z, [P, T], I32) for z in range(PASSES)]
+
+        def load_words(z):
+            nc.sync.dma_start(out=word_win[z][:], in_=x_words[z].rearrange("p n t -> p (n t)").bitcast(I32))
+
+        raw = {}
+
+        def load_weight(name, w, h):
+            for z in range(PASSES):
+                raw[name, h, z] = tile("raw_%s_%d_%d" % (name, h, z), [P, PACK, HALF], F32)
+                rows = w[z * K_PASS : (z + 1) * K_PASS, h * HALF : (h + 1) * HALF]
+                nc.sync.dma_start(out=raw[name, h, z][:], in_=rows.rearrange("(p j) c -> p j c", j=PACK))
+
+        hw_t = {}
+
+        def load_hw(h):
+            for f in range(2 * h, 2 * h + 2):
+                hw_t[f] = tile("hw%d" % f, [P, S], F32)
+                nc.sync.dma_start(out=hw_t[f][:], in_=hw[f * P : (f + 1) * P, :])
+
+        load_words(0)
+        load_weight("w2", w2, 0)
+        load_words(1)
+        load_weight("w2", w2, 1)
+        load_weight("w1", w1, 0)
+        load_weight("w1", w1, 1)
+        load_weight("w3", w3, 0)
+        load_hw(0)
+        load_weight("w3", w3, 1)
+        load_hw(1)
+
+        c0_t = [bank("c0T%d" % b, "bank%d" % b, [P, CELL_TILES, P]) for b in range(BLOCKS)]
+        for t in range(CELL_TILES):
+            neg_c0 = tile("neg_c0_%d" % t, [P, S], F32)
+            for u in range(2):
+                cols = slice(u * S // 2, (u + 1) * S // 2)
+                lists = par_t[:, u * LIST_COLS // 2 : (u + 1) * LIST_COLS // 2]
+                nc.vector.tensor_scalar(neg_c0[:, cols], cell_win[t][:].indirect(lists), -1.0, 0.0, ALU.mult, ALU.add)
+            for b in range(BLOCKS):
+                nc.tensor.transpose(c0_t[b][:, t, :], neg_c0[:, b * P : (b + 1) * P], ident[:])
+
+        x_scale = tile("x_scale", [P, S], U8)
+        nc.vector.tensor_copy(x_scale[:], scale_win[:].indirect(offs_t[:]))
+        x_code = [tile("x_code%d" % z, [P, S], U32) for z in range(PASSES)]
+
+        def gather_words(z):
+            nc.vector.tensor_copy(x_code[z][:], word_win[z][:].bitcast(U32).indirect(offs_t[:]))
+
+        code, scale = {}, {}
+
+        def quantise(name, h, on_vector=()):
+            for z in range(PASSES):
+                key = (name, h, z)
+                grouped = tile("grp_%s_%d_%d" % key, [P, HALF, PACK], BF16)
+                dst = grouped[:].rearrange("p (c i) j -> p c j i", i=4)
+                src = raw[key][:].rearrange("p j (c i) -> p c j i", i=4)
+                if z in on_vector:
+                    nc.vector.tensor_copy(dst, src)
+                else:
+                    nc.scalar.copy(dst, src)
+                code[key] = tile("code_%s_%d_%d" % key, [P, HALF], U32)
+                scale[key] = tile("scale_%s_%d_%d" % key, [P, HALF], U8)
+                nc.vector.quantize_mx(
+                    out=code[key][:].bitcast(FP8X4),
+                    scales=scale[key][:],
+                    in_=grouped[:].rearrange("p c j -> p (c j)"),
+                )
+
+        def product_beams_on_partitions(name, h, tags):
+            banks = []
+            for pair in range(BLOCKS // 2):
+                acc = bank("%s_acc_%d_%d" % (name, h, pair), tags[pair], [P, 2, HALF])
+                for i in range(2):
+                    cols = slice((2 * pair + i) * P, (2 * pair + i + 1) * P)
+                    for z in range(PASSES):
+                        nc.tensor.matmul_mx(
+                            out=acc[:, i, :],
+                            lhsT=x_code[z][:, cols].bitcast(FP8X4),
+                            lhsT_scale=x_scale[4 * z :, cols],
+                            rhs=code[name, h, z][:].bitcast(FP8X4),
+                            rhs_scale=scale[name, h, z][:],
+                            start=(z == 0),
+                            stop=(z == PASSES - 1),
+                        )
+                banks.append(acc)
+            return banks
+
+        gather_words(0)
+
+        groups = HALF // (CELL_TILES * RUN)
+        fg, kept = {}, {}
+        for h in range(HALVES):
+            quantise("w2", h, on_vector=(1,) if h == 1 else ())
+            if h == 0:
+                gather_words(1)
+            u2 = product_beams_on_partitions("w2", h, ("bank%d" % (4 + 2 * h), "bank%d" % (5 + 2 * h)))
+            for pair in range(BLOCKS // 2):
+                fg[h, pair] = tile("fg_%d_%d" % (h, pair), [P, 2, HALF], F32)
+                nc.scalar.activation(fg[h, pair][:], u2[pair][:], ACT.Sigmoid)
+            for b in range(BLOCKS):
+                kept[h, b] = tile("kept_%d_%d" % (h, b), [P, HALF], F32)
+                nc.vector.tensor_tensor(
+                    kept[h, b][:].rearrange("p (g t e) -> p g t e", t=CELL_TILES, e=RUN),
+                    c0_t[b][:, :, h * groups * RUN : (h + 1) * groups * RUN].rearrange("p t (g e) -> p g t e", e=RUN),
+                    fg[h, b // 2][:, b % 2, :].rearrange("p (g t e) -> p g t e", t=CELL_TILES, e=RUN),
+                    ALU.mult,
+                )
+
+        neg_cn = [bank("neg_cn_%d" % fb, "bank%d" % fb, [P, S]) for fb in range(4)]
+        for fb in range(4):
+            for b in range(BLOCKS):
+                nc.tensor.matmul(
+                    neg_cn[fb][:, b * P : (b + 1) * P], kept[fb // 2, b][:, (fb % 2) * P : (fb % 2 + 1) * P], ident[:],
+                    start=(b == 0), stop=False, is_transpose=True,
+                )
+
+        th = {}
+        for h in range(HALVES):
+            quantise("w1", h, on_vector=(1,))
+            y = product_beams_on_partitions("w1", h, ("bank%d" % (4 + 2 * h), "bank%d" % (5 + 2 * h)))
+            for pair in range(BLOCKS // 2):
+                fresh = tile("fresh_%d_%d" % (h, pair), [P, 2, HALF], F32)
+                nc.vector.scalar_tensor_tensor(fresh[:], fg[h, pair][:], 1.0, y[pair][:], ALU.subtract, ALU.mult)
+                for i in range(2):
+                    b = 2 * pair + i
+                    for f in range(2):
+                        nc.tensor.matmul(
+                            neg_cn[2 * h + f][:, b * P : (b + 1) * P], fresh[:, i, f * P : (f + 1) * P], ident[:],
+                            start=False, stop=(b == BLOCKS - 1), is_transpose=True,
+                        )
+            for fb in range(2 * h, 2 * h + 2):
+                th[fb] = tile("tanh%d" % fb, [P, S], F32)
+                nc.scalar.activation(th[fb][:], neg_cn[fb][:], ACT.Tanh, scale=-1.0)
+
+        for h in range(HALVES):
+            quantise("w3", h)
+            for f in range(2):
+                fb = 2 * h + f
+                cols = slice(f * P, (f + 1) * P)
+                u3 = bank("u3_%d" % fb, "bank%d" % (4 + fb), [P, S])
+                for z in range(PASSES):
+                    nc.tensor.matmul_mx(
+                        out=u3[:],
+                        lhsT=code["w3", h, z][:, cols].bitcast(FP8X4),
+                        lhsT_scale=scale["w3", h, z][:, cols],
+                        rhs=x_code[z][:].bitcast(FP8X4),
+                        rhs_scale=x_scale[4 * z :, :],
+                        start=(z == 0),
+                        stop=(z == PASSES - 1),
+                    )
+                diff = tile("diff%d" % fb, [P, S], F32)
+                nc.vector.tensor_tensor(diff[:], th[fb][:], hw_t[fb][:], ALU.subtract)
+                rg = tile("rg%d" % fb, [P, S], F32)
+                nc.scalar.activation(rg[:], u3[:], ACT.Sigmoid)
+                gated = tile("gated%d" % fb, [P, S], F32)
+                nc.vector.tensor_tensor(gated[:], rg[:], diff[:], ALU.mult)
+                res = tile("res%d" % fb, [P, S], F32)
+                nc.vector.tensor_tensor(res[:], gated[:], hw_t[fb][:], ALU.add)
+                nc.sync.dma_start(out=out[fb * P : (fb + 1) * P, :], in_=res[:])

@@ -45,61 +45,73 @@ def tile_picked_sru8_none_p_kernel(tc, x_words, x_scales, cell, w1, w2, w3, hw, 
 
         scale_win = tile("scale_win", [P, T], U8)
         nc.vector.memset(scale_win[:].bitcast(I32), 0)
-        for q in range(4):
-            nc.scalar.dma_start(
-                out=scale_win[32 * q : 32 * q + 4 * PASSES, :].bitcast(I32),
-                in_=x_scales[:, 4 * q : 4 * q + 4, :].bitcast(I32),
-            )
         ident = tile("ident", [P, P], F32)
         make_identity(nc, ident[:])
-
         warm_in = tile("warm_in", [P, 1], F32)
         warm_out = tile("warm_out", [P, 1], F32)
         nc.vector.memset(warm_in[:], 0.0)
         nc.scalar.activation(warm_out[:], warm_in[:], ACT.Sigmoid)
 
-        nc.sync.dma_start(par_t[:], par)
+        def load_scales():
+            for q in range(4):
+                nc.sync.dma_start(
+                    out=scale_win[32 * q : 32 * q + 4 * PASSES, :].bitcast(I32),
+                    in_=x_scales[:, 4 * q : 4 * q + 4, :].bitcast(I32),
+                )
+
         cell_rows = cell.rearrange("(g t e) j -> t g e j", t=CELL_TILES, e=RUN)
-        cell_win = []
-        for t in range(CELL_TILES):
-            win = tile("cell_win%d" % t, [P, S], F32)
-            nc.sync.dma_start(out=win[:], in_=cell_rows[t])
-            cell_win.append(win)
-        nc.sync.dma_start(offs_t[:], offs)
+        cell_win = [tile("cell_win%d" % t, [P, S], F32) for t in range(CELL_TILES)]
+
+        def load_cell(t):
+            nc.sync.dma_start(out=cell_win[t][:], in_=cell_rows[t])
 
         word_win = [tile("word_win%d" % z, [P, T], I32) for z in range(PASSES)]
 
         def load_words(z):
             nc.sync.dma_start(out=word_win[z][:], in_=x_words[z].rearrange("p n t -> p (n t)").bitcast(I32))
 
+        weights = {"w1": w1, "w2": w2, "w3": w3}
         raw = {}
 
-        def load_weight(name, w, h):
-            for z in range(PASSES):
-                raw[name, h, z] = tile("raw_%s_%d_%d" % (name, h, z), [P, PACK, HALF], F32)
-                rows = w[z * K_PASS : (z + 1) * K_PASS, h * HALF : (h + 1) * HALF]
-                nc.sync.dma_start(out=raw[name, h, z][:], in_=rows.rearrange("(p j) c -> p j c", j=PACK))
+        def load_weight(name, h, z):
+            raw[name, h, z] = tile("raw_%s_%d_%d" % (name, h, z), [P, PACK, HALF], F32)
+            rows = weights[name][z * K_PASS : (z + 1) * K_PASS, h * HALF : (h + 1) * HALF]
+            nc.sync.dma_start(out=raw[name, h, z][:], in_=rows.rearrange("(p j) c -> p j c", j=PACK))
 
-        hw_t = {}
+        hw_t = [tile("hw%d" % fb, [P, S], F32) for fb in range(4)]
 
-        def load_hw(h):
-            for f in range(2 * h, 2 * h + 2):
-                hw_t[f] = tile("hw%d" % f, [P, S], F32)
-                nc.sync.dma_start(out=hw_t[f][:], in_=hw[f * P : (f + 1) * P, :])
+        def load_hw(fb):
+            nc.sync.dma_start(out=hw_t[fb][:], in_=hw[fb * P : (fb + 1) * P, :])
 
+        nc.sync.dma_start(par_t[:], par)
+        load_cell(0)
+        load_cell(1)
+        load_scales()
+        nc.sync.dma_start(offs_t[:], offs)
+        load_weight("w2", 0, 0)
+        load_weight("w2", 0, 1)
         load_words(0)
-        load_weight("w2", w2, 0)
+        load_cell(2)
         load_words(1)
-        load_weight("w2", w2, 1)
-        load_weight("w1", w1, 0)
-        load_weight("w1", w1, 1)
-        load_weight("w3", w3, 0)
+        load_cell(3)
+        load_weight("w2", 1, 0)
+        load_weight("w2", 1, 1)
+        load_weight("w1", 0, 0)
+        load_weight("w1", 0, 1)
+        load_weight("w1", 1, 0)
+        load_weight("w1", 1, 1)
+        load_weight("w3", 0, 0)
+        load_weight("w3", 0, 1)
         load_hw(0)
-        load_weight("w3", w3, 1)
         load_hw(1)
+        load_weight("w3", 1, 0)
+        load_weight("w3", 1, 1)
+        load_hw(2)
+        load_hw(3)
 
         c0_t = [bank("c0T%d" % b, "bank%d" % b, [P, CELL_TILES, P]) for b in range(BLOCKS)]
-        for t in range(CELL_TILES):
+
+        def gather_cell(t):
             neg_c0 = tile("neg_c0_%d" % t, [P, S], F32)
             for u in range(2):
                 cols = slice(u * S // 2, (u + 1) * S // 2)
@@ -109,63 +121,67 @@ def tile_picked_sru8_none_p_kernel(tc, x_words, x_scales, cell, w1, w2, w3, hw, 
                 nc.tensor.transpose(c0_t[b][:, t, :], neg_c0[:, b * P : (b + 1) * P], ident[:])
 
         x_scale = tile("x_scale", [P, S], U8)
-        nc.vector.tensor_copy(x_scale[:], scale_win[:].indirect(offs_t[:]))
         x_code = [tile("x_code%d" % z, [P, S], U32) for z in range(PASSES)]
+
+        def gather_scales():
+            nc.vector.tensor_copy(x_scale[:], scale_win[:].indirect(offs_t[:]))
 
         def gather_words(z):
             nc.vector.tensor_copy(x_code[z][:], word_win[z][:].bitcast(U32).indirect(offs_t[:]))
 
         code, scale = {}, {}
 
-        def quantise(name, h, on_vector=()):
-            for z in range(PASSES):
-                key = (name, h, z)
-                grouped = tile("grp_%s_%d_%d" % key, [P, HALF, PACK], BF16)
-                dst = grouped[:].rearrange("p (c i) j -> p c j i", i=4)
-                src = raw[key][:].rearrange("p j (c i) -> p c j i", i=4)
-                if z in on_vector:
-                    nc.vector.tensor_copy(dst, src)
-                else:
-                    nc.scalar.copy(dst, src)
-                code[key] = tile("code_%s_%d_%d" % key, [P, HALF], U32)
-                scale[key] = tile("scale_%s_%d_%d" % key, [P, HALF], U8)
-                nc.vector.quantize_mx(
-                    out=code[key][:].bitcast(FP8X4),
-                    scales=scale[key][:],
-                    in_=grouped[:].rearrange("p c j -> p (c j)"),
-                )
+        def cast(engine, dst, src):
+            dst = dst.rearrange("p (c i) j -> p c j i", i=4)
+            src = src.rearrange("p j (c i) -> p c j i", i=4)
+            if engine == "V":
+                nc.vector.tensor_copy(dst, src)
+            elif engine == "G":
+                nc.gpsimd.tensor_scalar(dst, src, 1.0, 0.0, ALU.mult, ALU.add)
+            else:
+                nc.scalar.copy(dst, src)
 
-        def product_beams_on_partitions(name, h, tags):
-            banks = []
-            for pair in range(BLOCKS // 2):
-                acc = bank("%s_acc_%d_%d" % (name, h, pair), tags[pair], [P, 2, HALF])
-                for i in range(2):
-                    cols = slice((2 * pair + i) * P, (2 * pair + i + 1) * P)
-                    for z in range(PASSES):
-                        nc.tensor.matmul_mx(
-                            out=acc[:, i, :],
-                            lhsT=x_code[z][:, cols].bitcast(FP8X4),
-                            lhsT_scale=x_scale[4 * z :, cols],
-                            rhs=code[name, h, z][:].bitcast(FP8X4),
-                            rhs_scale=scale[name, h, z][:],
-                            start=(z == 0),
-                            stop=(z == PASSES - 1),
-                        )
-                banks.append(acc)
-            return banks
+        def quantise(name, h, z, on_vector):
+            key = (name, h, z)
+            code[key] = tile("code_%s_%d_%d" % key, [P, HALF], U32)
+            scale[key] = tile("scale_%s_%d_%d" % key, [P, HALF], U8)
+            grouped = tile("grp_%s_%d_%d" % key, [P, HALF, PACK], BF16)
+            if on_vector < HALF:
+                cast("S", grouped[:, on_vector:, :], raw[key][:, :, on_vector:])
+            if on_vector > 0:
+                cast("V", grouped[:, :on_vector, :], raw[key][:, :, :on_vector])
+            nc.vector.quantize_mx(
+                out=code[key][:].bitcast(FP8X4),
+                scales=scale[key][:],
+                in_=grouped[:].rearrange("p c j -> p (c j)"),
+            )
 
-        gather_words(0)
+        def product_beams_on_partitions(name, h, pair, tag):
+            acc = bank("%s_acc_%d_%d" % (name, h, pair), tag, [P, 2, HALF])
+            for i in range(2):
+                cols = slice((2 * pair + i) * P, (2 * pair + i + 1) * P)
+                for z in range(PASSES):
+                    nc.tensor.matmul_mx(
+                        out=acc[:, i, :],
+                        lhsT=x_code[z][:, cols].bitcast(FP8X4),
+                        lhsT_scale=x_scale[4 * z :, cols],
+                        rhs=code[name, h, z][:].bitcast(FP8X4),
+                        rhs_scale=scale[name, h, z][:],
+                        start=(z == 0),
+                        stop=(z == PASSES - 1),
+                    )
+            return acc
 
         groups = HALF // (CELL_TILES * RUN)
-        fg, kept = {}, {}
-        for h in range(HALVES):
-            quantise("w2", h, on_vector=(1,) if h == 1 else ())
-            if h == 0:
-                gather_words(1)
-            u2 = product_beams_on_partitions("w2", h, ("bank%d" % (4 + 2 * h), "bank%d" % (5 + 2 * h)))
+        fg, kept, neg_cn, th, rg, part = {}, {}, {}, {}, {}, {}
+
+        def forget_gate(h, tags):
             for pair in range(BLOCKS // 2):
+                u2 = product_beams_on_partitions("w2", h, pair, tags[pair])
                 fg[h, pair] = tile("fg_%d_%d" % (h, pair), [P, 2, HALF], F32)
-                nc.scalar.activation(fg[h, pair][:], u2[pair][:], ACT.Sigmoid)
+                nc.scalar.activation(fg[h, pair][:], u2[:], ACT.Sigmoid)
+
+        def keep_old(h):
             for b in range(BLOCKS):
                 kept[h, b] = tile("kept_%d_%d" % (h, b), [P, HALF], F32)
                 nc.vector.tensor_tensor(
@@ -175,21 +191,20 @@ def tile_picked_sru8_none_p_kernel(tc, x_words, x_scales, cell, w1, w2, w3, hw, 
                     ALU.mult,
                 )
 
-        neg_cn = [bank("neg_cn_%d" % fb, "bank%d" % fb, [P, S]) for fb in range(4)]
-        for fb in range(4):
-            for b in range(BLOCKS):
-                nc.tensor.matmul(
-                    neg_cn[fb][:, b * P : (b + 1) * P], kept[fb // 2, b][:, (fb % 2) * P : (fb % 2 + 1) * P], ident[:],
-                    start=(b == 0), stop=False, is_transpose=True,
-                )
+        def turn_kept(h, tags):
+            for f in range(2):
+                neg_cn[2 * h + f] = bank("neg_cn_%d" % (2 * h + f), tags[f], [P, S])
+                for b in range(BLOCKS):
+                    nc.tensor.matmul(
+                        neg_cn[2 * h + f][:, b * P : (b + 1) * P], kept[h, b][:, f * P : (f + 1) * P], ident[:],
+                        start=(b == 0), stop=False, is_transpose=True,
+                    )
 
-        th = {}
-        for h in range(HALVES):
-            quantise("w1", h, on_vector=(1,))
-            y = product_beams_on_partitions("w1", h, ("bank%d" % (4 + 2 * h), "bank%d" % (5 + 2 * h)))
+        def candidate(h, tags):
             for pair in range(BLOCKS // 2):
+                y = product_beams_on_partitions("w1", h, pair, tags[pair])
                 fresh = tile("fresh_%d_%d" % (h, pair), [P, 2, HALF], F32)
-                nc.vector.scalar_tensor_tensor(fresh[:], fg[h, pair][:], 1.0, y[pair][:], ALU.subtract, ALU.mult)
+                nc.vector.scalar_tensor_tensor(fresh[:], fg[h, pair][:], 1.0, y[:], ALU.subtract, ALU.mult)
                 for i in range(2):
                     b = 2 * pair + i
                     for f in range(2):
@@ -197,32 +212,84 @@ def tile_picked_sru8_none_p_kernel(tc, x_words, x_scales, cell, w1, w2, w3, hw, 
                             neg_cn[2 * h + f][:, b * P : (b + 1) * P], fresh[:, i, f * P : (f + 1) * P], ident[:],
                             start=False, stop=(b == BLOCKS - 1), is_transpose=True,
                         )
-            for fb in range(2 * h, 2 * h + 2):
-                th[fb] = tile("tanh%d" % fb, [P, S], F32)
-                nc.scalar.activation(th[fb][:], neg_cn[fb][:], ACT.Tanh, scale=-1.0)
 
-        for h in range(HALVES):
-            quantise("w3", h)
-            for f in range(2):
-                fb = 2 * h + f
-                cols = slice(f * P, (f + 1) * P)
-                u3 = bank("u3_%d" % fb, "bank%d" % (4 + fb), [P, S])
-                for z in range(PASSES):
-                    nc.tensor.matmul_mx(
-                        out=u3[:],
-                        lhsT=code["w3", h, z][:, cols].bitcast(FP8X4),
-                        lhsT_scale=scale["w3", h, z][:, cols],
-                        rhs=x_code[z][:].bitcast(FP8X4),
-                        rhs_scale=x_scale[4 * z :, :],
-                        start=(z == 0),
-                        stop=(z == PASSES - 1),
-                    )
-                diff = tile("diff%d" % fb, [P, S], F32)
-                nc.vector.tensor_tensor(diff[:], th[fb][:], hw_t[fb][:], ALU.subtract)
-                rg = tile("rg%d" % fb, [P, S], F32)
-                nc.scalar.activation(rg[:], u3[:], ACT.Sigmoid)
-                gated = tile("gated%d" % fb, [P, S], F32)
-                nc.vector.tensor_tensor(gated[:], rg[:], diff[:], ALU.mult)
-                res = tile("res%d" % fb, [P, S], F32)
-                nc.vector.tensor_tensor(res[:], gated[:], hw_t[fb][:], ALU.add)
-                nc.sync.dma_start(out=out[fb * P : (fb + 1) * P, :], in_=res[:])
+        def cell_tanh(fb):
+            th[fb] = tile("tanh%d" % fb, [P, S], F32)
+            nc.scalar.activation(th[fb][:], neg_cn[fb][:], ACT.Tanh, scale=-1.0)
+
+        def reset_gate(fb, tag):
+            h, cols = fb // 2, slice((fb % 2) * P, (fb % 2 + 1) * P)
+            u3 = bank("u3_%d" % fb, tag, [P, S])
+            for z in range(PASSES):
+                nc.tensor.matmul_mx(
+                    out=u3[:],
+                    lhsT=code["w3", h, z][:, cols].bitcast(FP8X4),
+                    lhsT_scale=scale["w3", h, z][:, cols],
+                    rhs=x_code[z][:].bitcast(FP8X4),
+                    rhs_scale=x_scale[4 * z :, :],
+                    start=(z == 0),
+                    stop=(z == PASSES - 1),
+                )
+            rg[fb] = tile("rg%d" % fb, [P, S], F32)
+            nc.scalar.activation(rg[fb][:], u3[:], ACT.Sigmoid)
+
+        def mix_first(fb):
+            part[fb] = tile("part%d" % fb, [P, S], F32)
+            nc.vector.tensor_tensor(part[fb][:], th[fb][:], hw_t[fb][:], ALU.subtract)
+
+        def mix_second(fb):
+            part[fb, 1] = tile("second%d" % fb, [P, S], F32)
+            nc.vector.tensor_tensor(part[fb, 1][:], rg[fb][:], part[fb][:], ALU.mult)
+
+        def mix_last(fb):
+            res = tile("res%d" % fb, [P, S], F32)
+            nc.vector.tensor_tensor(res[:], part[fb, 1][:], hw_t[fb][:], ALU.add)
+            nc.sync.dma_start(out=out[fb * P : (fb + 1) * P, :], in_=res[:])
+
+        gather_cell(0)
+        gather_cell(1)
+        gather_scales()
+        quantise("w2", 0, 0, 0)
+        quantise("w2", 0, 1, 0)
+        gather_words(0)
+        gather_words(1)
+        gather_cell(2)
+        gather_cell(3)
+        forget_gate(0, ("bank4", "bank5"))
+        quantise("w2", 1, 0, 128)
+        quantise("w2", 1, 1, 128)
+        forget_gate(1, ("bank6", "bank7"))
+        quantise("w1", 0, 0, 128)
+        quantise("w1", 0, 1, 128)
+        keep_old(0)
+        keep_old(1)
+        turn_kept(0, ("bank0", "bank1"))
+        candidate(0, ("bank4", "bank5"))
+        cell_tanh(0)
+        cell_tanh(1)
+        quantise("w1", 1, 0, 128)
+        quantise("w1", 1, 1, 128)
+        turn_kept(1, ("bank2", "bank3"))
+        candidate(1, ("bank6", "bank7"))
+        cell_tanh(2)
+        cell_tanh(3)
+        quantise("w3", 0, 0, 64)
+        quantise("w3", 0, 1, 64)
+        reset_gate(0, "bank4")
+        reset_gate(1, "bank5")
+        quantise("w3", 1, 0, 64)
+        quantise("w3", 1, 1, 128)
+        reset_gate(2, "bank6")
+        reset_gate(3, "bank7")
+        mix_first(0)
+        mix_first(1)
+        mix_second(0)
+        mix_second(1)
+        mix_last(0)
+        mix_last(1)
+        mix_first(2)
+        mix_first(3)
+        mix_second(2)
+        mix_second(3)
+        mix_last(2)
+        mix_last(3)

@@ -78,7 +78,18 @@ def tile_picked_sru8_none_p_kernel(tc, x_words, x_scales, cell, w1, w2, w3, hw, 
             rows = weights[name][z * K_PASS : (z + 1) * K_PASS, h * HALF : (h + 1) * HALF]
             nc.sync.dma_start(out=raw[name, h, z][:], in_=rows.rearrange("(p j) c -> p j c", j=PACK))
 
-        hw_t = [tile("hw%d" % fb, [P, S], F32) for fb in range(4)]
+        def load_weight_pass(name, z):
+            whole = tile("raw_%s_%d" % (name, z), [P, PACK, N], F32)
+            rows = weights[name][z * K_PASS : (z + 1) * K_PASS, :]
+            nc.sync.dma_start(out=whole[:], in_=rows.rearrange("(p j) c -> p j c", j=PACK))
+            for h in range(HALVES):
+                raw[name, h, z] = whole[:, :, h * HALF : (h + 1) * HALF]
+
+        hw_pair = [tile("hw%d" % h, [P, 2, S], F32) for h in range(HALVES)]
+        hw_t = [hw_pair[fb // 2][:, fb % 2, :] for fb in range(4)]
+
+        def load_hw_pair(h):
+            nc.sync.dma_start(out=hw_pair[h][:], in_=hw[h * HALF : (h + 1) * HALF, :].rearrange("(f p) j -> p f j", p=P))
 
         def load_hw(fb):
             nc.sync.dma_start(out=hw_t[fb][:], in_=hw[fb * P : (fb + 1) * P, :])
@@ -96,29 +107,23 @@ def tile_picked_sru8_none_p_kernel(tc, x_words, x_scales, cell, w1, w2, w3, hw, 
         load_cell(3)
         load_weight("w2", 1, 0)
         load_weight("w2", 1, 1)
-        load_weight("w1", 0, 0)
-        load_weight("w1", 0, 1)
-        load_weight("w1", 1, 0)
-        load_weight("w1", 1, 1)
-        load_weight("w3", 0, 0)
-        load_weight("w3", 0, 1)
-        load_hw(0)
-        load_hw(1)
-        load_weight("w3", 1, 0)
-        load_weight("w3", 1, 1)
-        load_hw(2)
-        load_hw(3)
+        load_weight_pass("w1", 0)
+        load_weight_pass("w1", 1)
+        load_weight_pass("w3", 0)
+        load_weight_pass("w3", 1)
+        load_hw_pair(0)
+        load_hw_pair(1)
 
-        c0_t = [bank("c0T%d" % b, "bank%d" % b, [P, CELL_TILES, P]) for b in range(BLOCKS)]
+        c0_t = [bank("c0T%d" % b, "bank%d" % b, [P, P // RUN, CELL_TILES, RUN]) for b in range(BLOCKS)]
 
         def gather_cell(t):
-            neg_c0 = tile("neg_c0_%d" % t, [P, S], F32)
+            c0 = tile("c0_%d" % t, [P, S], F32)
             for u in range(2):
                 cols = slice(u * S // 2, (u + 1) * S // 2)
                 lists = par_t[:, u * LIST_COLS // 2 : (u + 1) * LIST_COLS // 2]
-                nc.vector.tensor_scalar(neg_c0[:, cols], cell_win[t][:].indirect(lists), -1.0, 0.0, ALU.mult, ALU.add)
+                nc.vector.tensor_copy(c0[:, cols], cell_win[t][:].indirect(lists))
             for b in range(BLOCKS):
-                nc.tensor.transpose(c0_t[b][:, t, :], neg_c0[:, b * P : (b + 1) * P], ident[:])
+                nc.tensor.transpose(c0_t[b][:, :, t, :], c0[:, b * P : (b + 1) * P], ident[:])
 
         x_scale = tile("x_scale", [P, S], U8)
         x_code = [tile("x_code%d" % z, [P, S], U32) for z in range(PASSES)]
@@ -172,24 +177,19 @@ def tile_picked_sru8_none_p_kernel(tc, x_words, x_scales, cell, w1, w2, w3, hw, 
                     )
             return acc
 
-        groups = HALF // (CELL_TILES * RUN)
         fg, kept, neg_cn, th, rg, part = {}, {}, {}, {}, {}, {}
 
         def forget_gate(h, tags):
             for pair in range(BLOCKS // 2):
                 u2 = product_beams_on_partitions("w2", h, pair, tags[pair])
                 fg[h, pair] = tile("fg_%d_%d" % (h, pair), [P, 2, HALF], F32)
-                nc.scalar.activation(fg[h, pair][:], u2[:], ACT.Sigmoid)
+                nc.scalar.activation(fg[h, pair][:], u2[:], ACT.Sigmoid, scale=-1.0)
 
         def keep_old(h):
             for b in range(BLOCKS):
                 kept[h, b] = tile("kept_%d_%d" % (h, b), [P, HALF], F32)
-                nc.vector.tensor_tensor(
-                    kept[h, b][:].rearrange("p (g t e) -> p g t e", t=CELL_TILES, e=RUN),
-                    c0_t[b][:, :, h * groups * RUN : (h + 1) * groups * RUN].rearrange("p t (g e) -> p g t e", e=RUN),
-                    fg[h, b // 2][:, b % 2, :].rearrange("p (g t e) -> p g t e", t=CELL_TILES, e=RUN),
-                    ALU.mult,
-                )
+                old = c0_t[b][:].rearrange("p g t e -> p (g t e)")[:, h * HALF : (h + 1) * HALF]
+                nc.vector.scalar_tensor_tensor(kept[h, b][:], fg[h, b // 2][:, b % 2, :], 1.0, old, ALU.subtract, ALU.mult)
 
         def turn_kept(h, tags):
             for f in range(2):
@@ -204,7 +204,7 @@ def tile_picked_sru8_none_p_kernel(tc, x_words, x_scales, cell, w1, w2, w3, hw, 
             for pair in range(BLOCKS // 2):
                 y = product_beams_on_partitions("w1", h, pair, tags[pair])
                 fresh = tile("fresh_%d_%d" % (h, pair), [P, 2, HALF], F32)
-                nc.vector.scalar_tensor_tensor(fresh[:], fg[h, pair][:], 1.0, y[:], ALU.subtract, ALU.mult)
+                nc.vector.scalar_tensor_tensor(fresh[:], y[:], -1.0, fg[h, pair][:], ALU.mult, ALU.mult)
                 for i in range(2):
                     b = 2 * pair + i
                     for f in range(2):
@@ -259,10 +259,10 @@ def tile_picked_sru8_none_p_kernel(tc, x_words, x_scales, cell, w1, w2, w3, hw, 
         quantise("w2", 1, 0, 128)
         quantise("w2", 1, 1, 128)
         forget_gate(1, ("bank6", "bank7"))
-        quantise("w1", 0, 0, 128)
-        quantise("w1", 0, 1, 128)
         keep_old(0)
         keep_old(1)
+        quantise("w1", 0, 0, 128)
+        quantise("w1", 0, 1, 128)
         turn_kept(0, ("bank0", "bank1"))
         candidate(0, ("bank4", "bank5"))
         cell_tanh(0)
@@ -283,12 +283,12 @@ def tile_picked_sru8_none_p_kernel(tc, x_words, x_scales, cell, w1, w2, w3, hw, 
         reset_gate(3, "bank7")
         mix_first(0)
         mix_first(1)
+        mix_first(2)
+        mix_first(3)
         mix_second(0)
         mix_second(1)
         mix_last(0)
         mix_last(1)
-        mix_first(2)
-        mix_first(3)
         mix_second(2)
         mix_second(3)
         mix_last(2)

@@ -97,20 +97,24 @@ def tile_picked_sru8_none_p_kernel(tc, x_words, x_scales, cell, w1, w2, w3, hw, 
         nc.sync.dma_start(par_t[:], par)
         load_cell(0)
         load_cell(1)
-        load_scales()
         nc.sync.dma_start(offs_t[:], offs)
-        load_weight("w2", 0, 0)
-        load_weight("w2", 0, 1)
+        load_scales()
         load_words(0)
+        load_weight("w2", 0, 0)
         load_cell(2)
         load_words(1)
+        load_weight("w2", 0, 1)
         load_cell(3)
         load_weight("w2", 1, 0)
         load_weight("w2", 1, 1)
-        load_weight_pass("w1", 0)
-        load_weight_pass("w1", 1)
-        load_weight_pass("w3", 0)
-        load_weight_pass("w3", 1)
+        load_weight("w1", 0, 0)
+        load_weight("w1", 0, 1)
+        load_weight("w1", 1, 0)
+        load_weight("w1", 1, 1)
+        load_weight("w3", 0, 0)
+        load_weight("w3", 0, 1)
+        load_weight("w3", 1, 0)
+        load_weight("w3", 1, 1)
         load_hw_pair(0)
         load_hw_pair(1)
 
@@ -194,24 +198,24 @@ def tile_picked_sru8_none_p_kernel(tc, x_words, x_scales, cell, w1, w2, w3, hw, 
         def turn_kept(h, tags):
             for f in range(2):
                 neg_cn[2 * h + f] = bank("neg_cn_%d" % (2 * h + f), tags[f], [P, S])
-                for b in range(BLOCKS):
-                    nc.tensor.matmul(
-                        neg_cn[2 * h + f][:, b * P : (b + 1) * P], kept[h, b][:, f * P : (f + 1) * P], ident[:],
-                        start=(b == 0), stop=False, is_transpose=True,
-                    )
+
+        y = {}
 
         def candidate(h, tags):
             for pair in range(BLOCKS // 2):
-                y = product_beams_on_partitions("w1", h, pair, tags[pair])
+                y[h, pair] = product_beams_on_partitions("w1", h, pair, tags[pair])
+
+        def new_cell(h):
+            for pair in range(BLOCKS // 2):
                 fresh = tile("fresh_%d_%d" % (h, pair), [P, 2, HALF], F32)
-                nc.vector.scalar_tensor_tensor(fresh[:], y[:], -1.0, fg[h, pair][:], ALU.mult, ALU.mult)
+                nc.vector.scalar_tensor_tensor(fresh[:], y[h, pair][:], -1.0, fg[h, pair][:], ALU.mult, ALU.mult)
                 for i in range(2):
                     b = 2 * pair + i
                     for f in range(2):
-                        nc.tensor.matmul(
-                            neg_cn[2 * h + f][:, b * P : (b + 1) * P], fresh[:, i, f * P : (f + 1) * P], ident[:],
-                            start=False, stop=(b == BLOCKS - 1), is_transpose=True,
-                        )
+                        cols = slice(f * P, (f + 1) * P)
+                        target = neg_cn[2 * h + f][:, b * P : (b + 1) * P]
+                        nc.tensor.matmul(target, fresh[:, i, cols], ident[:], start=True, stop=False, is_transpose=True)
+                        nc.tensor.matmul(target, kept[h, b][:, cols], ident[:], start=False, stop=True, is_transpose=True)
 
         def cell_tanh(fb):
             th[fb] = tile("tanh%d" % fb, [P, S], F32)
@@ -246,39 +250,41 @@ def tile_picked_sru8_none_p_kernel(tc, x_words, x_scales, cell, w1, w2, w3, hw, 
             nc.vector.tensor_tensor(res[:], part[fb, 1][:], hw_t[fb][:], ALU.add)
             nc.sync.dma_start(out=out[fb * P : (fb + 1) * P, :], in_=res[:])
 
-        gather_cell(0)
-        gather_cell(1)
         gather_scales()
-        quantise("w2", 0, 0, 0)
-        quantise("w2", 0, 1, 0)
         gather_words(0)
         gather_words(1)
+        quantise("w2", 0, 0, 0)
+        quantise("w2", 0, 1, 256)
+        forget_gate(0, ("bank4", "bank5"))
+        quantise("w2", 1, 0, 0)
+        quantise("w2", 1, 1, 256)
+        forget_gate(1, ("bank6", "bank7"))
+        quantise("w1", 0, 0, 0)
+        quantise("w1", 0, 1, 256)
+        candidate(0, ("bank4", "bank5"))
+        quantise("w1", 1, 0, 0)
+        quantise("w1", 1, 1, 256)
+        candidate(1, ("bank6", "bank7"))
+        gather_cell(0)
+        gather_cell(1)
         gather_cell(2)
         gather_cell(3)
-        forget_gate(0, ("bank4", "bank5"))
-        quantise("w2", 1, 0, 128)
-        quantise("w2", 1, 1, 128)
-        forget_gate(1, ("bank6", "bank7"))
         keep_old(0)
         keep_old(1)
-        quantise("w1", 0, 0, 128)
-        quantise("w1", 0, 1, 128)
         turn_kept(0, ("bank0", "bank1"))
-        candidate(0, ("bank4", "bank5"))
+        new_cell(0)
         cell_tanh(0)
         cell_tanh(1)
-        quantise("w1", 1, 0, 128)
-        quantise("w1", 1, 1, 128)
         turn_kept(1, ("bank2", "bank3"))
-        candidate(1, ("bank6", "bank7"))
+        new_cell(1)
         cell_tanh(2)
         cell_tanh(3)
-        quantise("w3", 0, 0, 64)
-        quantise("w3", 0, 1, 64)
+        quantise("w3", 0, 0, 0)
+        quantise("w3", 0, 1, 0)
+        quantise("w3", 1, 0, 0)
+        quantise("w3", 1, 1, 128)
         reset_gate(0, "bank4")
         reset_gate(1, "bank5")
-        quantise("w3", 1, 0, 64)
-        quantise("w3", 1, 1, 128)
         reset_gate(2, "bank6")
         reset_gate(3, "bank7")
         mix_first(0)

from contextlib import ExitStack

import concourse.mybir as mybir
from concourse.masks import make_identity

K, T, S, N = 1024, 2048, 512, 512
FLOPS = 3 * 2 * K * S * N

F32 = mybir.dt.float32
BF16 = mybir.dt.bfloat16
I32 = mybir.dt.int32
U32 = mybir.dt.uint32
U16 = mybir.dt.uint16
U8 = mybir.dt.uint8
FP8X4 = mybir.dt.float8_e4m3fn_x4
ALU = mybir.AluOpType
ACT = mybir.ActivationFunctionType

P = 128
PACK = 4
K_PASS = P * PACK
PASSES = K // K_PASS
HALVES = 2
HALF = N // HALVES
BLOCKS = S // P
CELL_TILES = N // P
RUN = 4
LIST_COLS = S // 16


def tile_picked_sru8_none_p_kernel(tc, x_words, x_scales, cell, w1, w2, w3, hw, offs, par, out):
    nc = tc.nc
    with ExitStack() as ctx:
        sb = ctx.enter_context(tc.tile_pool(name="sb", bufs=1))
        ps = ctx.enter_context(tc.psum_pool(name="ps", bufs=1))

        def tile(name, shape, dtype):
            return sb.tile(shape, dtype, name=name, align_bytes=64)

        def bank(name, tag, shape):
            return ps.tile(shape, F32, name=name, tag=tag)

        par_t = sb.tile([P, LIST_COLS], U16, name="par_t")
        offs_t = sb.tile([P, LIST_COLS], U16, name="offs_t")

        scale_win = tile("scale_win", [P, T], U8)
        nc.vector.memset(scale_win[:].bitcast(I32), 0)
        ident = tile("ident", [P, P], F32)
        make_identity(nc, ident[:])
        warm_in = tile("warm_in", [P, 1], F32)
        warm_out = tile("warm_out", [P, 1], F32)
        nc.vector.memset(warm_in[:], 0.0)
        nc.scalar.activation(warm_out[:], warm_in[:], ACT.Sigmoid)

        def load_scales():
            for q in range(4):
                nc.sync.dma_start(
                    out=scale_win[32 * q : 32 * q + 4 * PASSES, :].bitcast(I32),
                    in_=x_scales[:, 4 * q : 4 * q + 4, :].bitcast(I32),
                )

        cell_rows = cell.rearrange("(g t e) j -> t g e j", t=CELL_TILES, e=RUN)
        cell_win = [tile("cell_win%d" % t, [P, S], F32) for t in range(CELL_TILES)]

        def load_cell(t):
            nc.sync.dma_start(out=cell_win[t][:], in_=cell_rows[t])

        word_win = [tile("word_win%d" % z, [P, T], I32) for z in range(PASSES)]

        def load_words(z):
            nc.sync.dma_start(out=word_win[z][:], in_=x_words[z].rearrange("p n t -> p (n t)").bitcast(I32))

        weights = {"w1": w1, "w2": w2, "w3": w3}
        raw = {}

        def load_weight(name, h, z):
            raw[name, h, z] = tile("raw_%s_%d_%d" % (name, h, z), [P, PACK, HALF], F32)
            rows = weights[name][z * K_PASS : (z + 1) * K_PASS, h * HALF : (h + 1) * HALF]
            nc.sync.dma_start(out=raw[name, h, z][:], in_=rows.rearrange("(p j) c -> p j c", j=PACK))

        def load_weight_pass(name, z):
            whole = tile("raw_%s_%d" % (name, z), [P, PACK, N], F32)
            rows = weights[name][z * K_PASS : (z + 1) * K_PASS, :]
            nc.sync.dma_start(out=whole[:], in_=rows.rearrange("(p j) c -> p j c", j=PACK))
            for h in range(HALVES):
                raw[name, h, z] = whole[:, :, h * HALF : (h + 1) * HALF]

        hw_pair = [tile("hw%d" % h, [P, 2, S], F32) for h in range(HALVES)]
        hw_t = [hw_pair[fb // 2][:, fb % 2, :] for fb in range(4)]

        def load_hw_pair(h):
            nc.sync.dma_start(out=hw_pair[h][:], in_=hw[h * HALF : (h + 1) * HALF, :].rearrange("(f p) j -> p f j", p=P))

        def load_hw(fb):
            nc.sync.dma_start(out=hw_t[fb][:], in_=hw[fb * P : (fb + 1) * P, :])

        nc.sync.dma_start(par_t[:], par)
        load_cell(0)
        load_cell(1)
        nc.sync.dma_start(offs_t[:], offs)
        load_scales()
        load_words(0)
        load_weight("w2", 0, 0)
        load_cell(2)
        load_words(1)
        load_weight("w2", 0, 1)
        load_cell(3)
        load_weight("w2", 1, 0)
        load_weight("w2", 1, 1)
        load_weight("w1", 0, 0)
        load_weight("w1", 0, 1)
        load_weight("w1", 1, 0)
        load_weight("w1", 1, 1)
        load_weight("w3", 0, 0)
        load_weight("w3", 0, 1)
        load_weight("w3", 1, 0)
        load_weight("w3", 1, 1)
        load_hw_pair(0)
        load_hw_pair(1)

        c0_t = [bank("c0T%d" % b, "bank%d" % b, [P, P // RUN, CELL_TILES, RUN]) for b in range(BLOCKS)]

        def gather_cell(t):
            c0 = tile("c0_%d" % t, [P, S], F32)
            for u in range(2):
                cols = slice(u * S // 2, (u + 1) * S // 2)
                lists = par_t[:, u * LIST_COLS // 2 : (u + 1) * LIST_COLS // 2]
                nc.vector.tensor_copy(c0[:, cols], cell_win[t][:].indirect(lists))
            for b in range(BLOCKS):
                nc.tensor.transpose(c0_t[b][:, :, t, :], c0[:, b * P : (b + 1) * P], ident[:])

        x_scale = tile("x_scale", [P, S], U8)
        x_code = [tile("x_code%d" % z, [P, S], U32) for z in range(PASSES)]

        def gather_scales():
            nc.vector.tensor_copy(x_scale[:], scale_win[:].indirect(offs_t[:]))

        def gather_words(z):
            nc.vector.tensor_copy(x_code[z][:], word_win[z][:].bitcast(U32).indirect(offs_t[:]))

        code, scale = {}, {}

        def cast(engine, dst, src):
            dst = dst.rearrange("p (c i) j -> p c j i", i=4)
            src = src.rearrange("p j (c i) -> p c j i", i=4)
            if engine == "V":
                nc.vector.tensor_copy(dst, src)
            elif engine == "G":
                nc.gpsimd.tensor_scalar(dst, src, 1.0, 0.0, ALU.mult, ALU.add)
            else:
                nc.scalar.copy(dst, src)

        def quantise(name, h, z, on_vector):
            key = (name, h, z)
            code[key] = tile("code_%s_%d_%d" % key, [P, HALF], U32)
            scale[key] = tile("scale_%s_%d_%d" % key, [P, HALF], U8)
            grouped = tile("grp_%s_%d_%d" % key, [P, HALF, PACK], BF16)
            if on_vector < HALF:
                cast("S", grouped[:, on_vector:, :], raw[key][:, :, on_vector:])
            if on_vector > 0:
                cast("V", grouped[:, :on_vector, :], raw[key][:, :, :on_vector])
            nc.vector.quantize_mx(
                out=code[key][:].bitcast(FP8X4),
                scales=scale[key][:],
                in_=grouped[:].rearrange("p c j -> p (c j)"),
            )

        def product_beams_on_partitions(name, h, pair, tag):
            acc = bank("%s_acc_%d_%d" % (name, h, pair), tag, [P, 2, HALF])
            for i in range(2):
                cols = slice((2 * pair + i) * P, (2 * pair + i + 1) * P)
                for z in range(PASSES):
                    nc.tensor.matmul_mx(
                        out=acc[:, i, :],
                        lhsT=x_code[z][:, cols].bitcast(FP8X4),
                        lhsT_scale=x_scale[4 * z :, cols],
                        rhs=code[name, h, z][:].bitcast(FP8X4),
                        rhs_scale=scale[name, h, z][:],
                        start=(z == 0),
                        stop=(z == PASSES - 1),
                    )
            return acc

        fg, kept, neg_cn, th, rg, part = {}, {}, {}, {}, {}, {}

        def forget_gate(h, tags):
            for pair in range(BLOCKS // 2):
                u2 = product_beams_on_partitions("w2", h, pair, tags[pair])
                fg[h, pair] = tile("fg_%d_%d" % (h, pair), [P, 2, HALF], F32)
                nc.scalar.activation(fg[h, pair][:], u2[:], ACT.Sigmoid, scale=-1.0)

        def keep_old(h):
            for b in range(BLOCKS):
                kept[h, b] = tile("kept_%d_%d" % (h, b), [P, HALF], F32)
                old = c0_t[b][:].rearrange("p g t e -> p (g t e)")[:, h * HALF : (h + 1) * HALF]
                nc.vector.scalar_tensor_tensor(kept[h, b][:], fg[h, b // 2][:, b % 2, :], 1.0, old, ALU.subtract, ALU.mult)

        def turn_kept(h, tags):
            for f in range(2):
                neg_cn[2 * h + f] = bank("neg_cn_%d" % (2 * h + f), tags[f], [P, S])

        y = {}

        def candidate(h, tags):
            for pair in range(BLOCKS // 2):
                y[h, pair] = product_beams_on_partitions("w1", h, pair, tags[pair])

        def new_cell(h):
            for pair in range(BLOCKS // 2):
                fresh = tile("fresh_%d_%d" % (h, pair), [P, 2, HALF], F32)
                nc.vector.scalar_tensor_tensor(fresh[:], y[h, pair][:], -1.0, fg[h, pair][:], ALU.mult, ALU.mult)
                for i in range(2):
                    b = 2 * pair + i
                    for f in range(2):
                        cols = slice(f * P, (f + 1) * P)
                        target = neg_cn[2 * h + f][:, b * P : (b + 1) * P]
                        nc.tensor.matmul(target, fresh[:, i, cols], ident[:], start=True, stop=False, is_transpose=True)
                        nc.tensor.matmul(target, kept[h, b][:, cols], ident[:], start=False, stop=True, is_transpose=True)

        def cell_tanh(fb):
            th[fb] = tile("tanh%d" % fb, [P, S], F32)
            nc.scalar.activation(th[fb][:], neg_cn[fb][:], ACT.Tanh, scale=-1.0)

        def reset_gate(fb, tag):
            h, cols = fb // 2, slice((fb % 2) * P, (fb % 2 + 1) * P)
            u3 = bank("u3_%d" % fb, tag, [P, S])
            for z in range(PASSES):
                nc.tensor.matmul_mx(
                    out=u3[:],
                    lhsT=code["w3", h, z][:, cols].bitcast(FP8X4),
                    lhsT_scale=scale["w3", h, z][:, cols],
                    rhs=x_code[z][:].bitcast(FP8X4),
                    rhs_scale=x_scale[4 * z :, :],
                    start=(z == 0),
                    stop=(z == PASSES - 1),
                )
            rg[fb] = tile("rg%d" % fb, [P, S], F32)
            nc.scalar.activation(rg[fb][:], u3[:], ACT.Sigmoid)

        def mix_first(fb):
            part[fb] = tile("part%d" % fb, [P, S], F32)
            nc.vector.tensor_tensor(part[fb][:], th[fb][:], hw_t[fb][:], ALU.subtract)

        def mix_second(fb):
            part[fb, 1] = tile("second%d" % fb, [P, S], F32)
            nc.vector.tensor_tensor(part[fb, 1][:], rg[fb][:], part[fb][:], ALU.mult)

        def mix_last(fb):
            res = tile("res%d" % fb, [P, S], F32)
            nc.vector.tensor_tensor(res[:], part[fb, 1][:], hw_t[fb][:], ALU.add)
            nc.sync.dma_start(out=out[fb * P : (fb + 1) * P, :], in_=res[:])

        gather_scales()
        gather_words(0)
        gather_words(1)
        quantise("w2", 0, 0, 0)
        quantise("w2", 0, 1, 256)
        forget_gate(0, ("bank4", "bank5"))
        quantise("w2", 1, 0, 0)
        quantise("w2", 1, 1, 256)
        forget_gate(1, ("bank6", "bank7"))
        quantise("w1", 0, 0, 0)
        quantise("w1", 0, 1, 256)
        candidate(0, ("bank4", "bank5"))
        quantise("w1", 1, 0, 0)
        quantise("w1", 1, 1, 256)
        candidate(1, ("bank6", "bank7"))
        gather_cell(0)
        gather_cell(1)
        gather_cell(2)
        gather_cell(3)
        keep_old(0)
        keep_old(1)
        turn_kept(0, ("bank0", "bank1"))
        new_cell(0)
        cell_tanh(0)
        cell_tanh(1)
        turn_kept(1, ("bank2", "bank3"))
        new_cell(1)
        cell_tanh(2)
        cell_tanh(3)
        quantise("w3", 0, 0, 0)
        quantise("w3", 0, 1, 0)
        quantise("w3", 1, 0, 0)
        quantise("w3", 1, 1, 128)
        reset_gate(0, "bank4")
        reset_gate(1, "bank5")
        reset_gate(2, "bank6")
        reset_gate(3, "bank7")
        mix_first(0)
        mix_first(1)
        mix_first(2)
        mix_first(3)
        mix_second(0)
        mix_second(1)
        mix_last(0)
        mix_last(1)
        mix_second(2)
        mix_second(3)
        mix_last(2)
        mix_last(3)
